import numpy as np
CORES = [211,219,227,235,243,251,83,91,99,107,115,123]
N = 12
TIMES = 2
def setup_inputs(rng):
    x = (rng.standard_normal((N, 128, 128), dtype=np.float32) / np.float32(np.sqrt(512 * N)))
    return {"x": x, "xt": x.transpose(0, 2, 1).copy()}
def setup_inputs_big(rng):
    d = setup_inputs(rng)
    for k in ("x", "xt"): d[k] = (d[k].astype(np.float32) * 1024.0).astype(d[k].dtype)
    return d
def setup_inputs_small(rng):
    d = setup_inputs(rng)
    for k in ("x", "xt"): d[k] = (d[k].astype(np.float32) * (1 / 1024.0)).astype(d[k].dtype)
    return d
def setup_inputs_apart(rng):
    d = setup_inputs(rng)
    f = (10.0 ** rng.permutation(np.linspace(-1.5, 1.5, N))).astype(np.float32).reshape(N, 1, 1)
    for k in ("x", "xt"): d[k] = (d[k].astype(np.float32) * f).astype(d[k].dtype)
    return d
def reference(x, xt):
    X = list(x.astype(np.float64))
    for _ in range(TIMES):
        G = sum(a.T @ a for a in X)
        X = [1.5 * a - 0.5 * (a @ G) for a in X]
    return {"y": np.stack(X).astype(np.float32)}

@@ -1,0 +1,251 @@
+from concourse.bass import DstId, RemoteDMATransfer
+from concourse.mybir import AluOpType
+
+P = 128
+SHAPE = ("quad", "trio")
+_SIZE = {"mate": 2, "twin": 2, "trio": 3, "quad": 4, "plane": 6, "all": 12}
+ENGINES = 8
+
+SCRATCH = {
+    "xin": ("sbuf", [P, P * _SIZE[SHAPE[0]]], "float32"),
+    "xts": ("sbuf", [P, P], "float32"),
+    "xt16": ("sbuf", [P, P], "float32"),
+    "c16": ("sbuf", [P, P], "float32"),
+    "sd": ("sbuf", [P, P + 1], "float32"),
+    "i3": ("sbuf", [P, P], "float32"),
+    "i6": ("sbuf", [P, P], "float32"),
+    "i12": ("sbuf", [P, P], "float32"),
+    "a_sb": ("sbuf", [P, P], "float32"),
+    "g_sb": ("sbuf", [P, P], "float32"),
+    "b_sb": ("sbuf", [P, P], "float32"),
+    "ut_sb": ("sbuf", [P, P], "float32"),
+    "d_sb": ("sbuf", [P, P], "float32"),
+    "y_sb": ("sbuf", [P, P], "float32"),
+    "da": ("dram", [P, P + 1], "float32"),
+    "db": ("dram", [P + 1, P], "float32"),
+    "gq": ("psum", [P, 512], "float32"),
+    "acc": ("psum", [P, 512], "float32"),
+    "b_ps": ("psum", [P, 512], "float32"),
+    "ut_ps": ("psum", [P, 512], "float32"),
+    "c_ps": ("psum", [P, 512], "float32"),
+    "y_ps": ("psum", [P, 512], "float32"),
+}
+SEMAPHORES = ["sx", "sxt", "si3", "sout", "left"]
+SEMAPHORES += ["a%d" % j for j in range(_SIZE[SHAPE[0]])]
+for _k, _kind in enumerate(SHAPE[1:]):
+    SCRATCH["gin%d" % _k] = ("sbuf", [P, P * _SIZE[_kind]], "float32")
+    SEMAPHORES += ["b%d_%d" % (_k, j) for j in range(_SIZE[_kind])]
+SEMAPHORES += ["p%d" % j for j in range(40)]
+
+
+def _members(kind, c, ranks, topo):
+    def mate(a):
+        return [r for r in ranks if r == a or topo.mates(a, r)]
+
+    def twin(a):
+        return [r for r in ranks if topo.chip(r) == topo.chip(a)]
+
+    if kind == "mate":
+        return mate(c)
+    if kind == "twin":
+        return twin(c)
+    if kind == "quad":
+        both = [t for m in mate(c) for t in twin(m)]
+        return [r for r in ranks if r in both]
+    if kind == "trio":
+        return [r for r in ranks if r == c or (topo.same_plane(c, r) and topo.host(r) == topo.host(c))]
+    if kind == "plane":
+        return [r for r in ranks if r == c or topo.same_plane(c, r)]
+    return list(ranks)
+
+
+def _far(topo, a, b):
+    if topo.mates(a, b):
+        return 2
+    if topo.same_plane(a, b):
+        return 1
+    return 0
+
+
+def _send_order(topo, mem, c):
+    n = len(mem)
+    return sorted([p for p in mem if p != c], key=lambda p: (_far(topo, c, p), (mem.index(p) - mem.index(c)) % n))
+
+
+def _recv_order(topo, mem, c):
+    n = len(mem)
+    return sorted([p for p in mem if p != c], key=lambda p: (_far(topo, p, c), (mem.index(c) - mem.index(p)) % n))
+
+
+def _mask(topo, mem, c):
+    m = -1
+    for p in mem:
+        if p != c:
+            m &= topo.mask(c, p)
+    out, bit, n = 0, 1, 0
+    while n < ENGINES and bit <= m:
+        if m & bit:
+            out |= bit
+            n += 1
+        bit <<= 1
+    return out
+
+
+def _count(m):
+    return bin(m).count("1")
+
+
+def rank_program(g, core, T, topo):
+    if T.rank_of(core) is None:
+        return
+    ranks = list(T.cores)
+    sem = T.sem
+    ten, vec, syn, sca = g.tensor, g.vector, g.sync, g.scalar
+    add, sub, mult = AluOpType.add, AluOpType.subtract, AluOpType.mult
+    used = [0]
+    left = [0]
+    slot = [0]
+
+    def new_sem():
+        used[0] += 1
+        return sem["p%d" % (used[0] - 1)]
+
+    def col(buf, j):
+        return buf[:, j * P:(j + 1) * P]
+
+    def acc_slot():
+        slot[0] += 1
+        return col(T.acc, (slot[0] - 1) % 4)
+
+    def send(buf, mem, name):
+        me = mem.index(core)
+        m = _mask(topo, mem, core)
+        peers = _send_order(topo, mem, core)
+        dests = []
+        for p in peers:
+            assert topo.may_write(core, p)
+            rid, pid = topo.addr(p, core)
+            dests.append(DstId(rid=rid, pnc=pid))
+        g.remote_dma_fused(
+            [RemoteDMATransfer(dst_ids=dests, dma_engine_mask=m, remote_sem=sem[name % me],
+                               srcs=[col(buf, me)], dsts=[col(buf, me) for p in peers])],
+            local_sem=sem.left)
+        left[0] += _count(m)
+
+    xmem = _members(SHAPE[0], core, ranks, topo)
+    gmem = [_members(kind, core, ranks, topo) for kind in SHAPE[1:]]
+    xme = xmem.index(core)
+    xown = col(T.xin, xme)
+
+    syn.dma_start(xown, T.x[:, :]).then_inc(sem.sx, 16)
+    m0, m1, mc, d1, d2 = new_sem(), new_sem(), new_sem(), new_sem(), new_sem()
+    vec.memset(T.sd[:, :], 0.0).then_inc(m0, 1)
+    vec.memset(T.c16[:, :], 0.0625).then_inc(mc, 1)
+    vec.wait_ge(m0, 1)
+    vec.memset(T.sd[:, 0:1], 3.0).then_inc(m1, 1)
+    sca.wait_ge(sem.sx, 16)
+    sca.dma_start(T.xts[:, :], T.xt[:, :]).then_inc(sem.sxt, 16)
+    sca.wait_ge(m1, 1)
+    sca.dma_start(T.da[:, :], T.sd[:, :]).then_inc(d1, 16)
+    sca.wait_ge(d1, 16)
+    sca.dma_start(T.db[:, :], T.da[:, :]).then_inc(d2, 16)
+    sca.wait_ge(d2, 16)
+    sca.dma_start(T.i3[:, :], T.db[0:P, :]).then_inc(sem.si3, 16)
+
+    g.wait_ge(sem.sx, 16)
+    if len(xmem) > 1:
+        send(T.xin, xmem, "a%d")
+
+    t_gq = new_sem()
+    gq = T.gq[:, 0:P]
+    rec = _recv_order(topo, xmem, core)
+    ten.wait_ge(sem.sx, 16)
+    mm = ten.matmul(gq, xown, xown, True, not rec)
+    for j, p in enumerate(rec):
+        ten.wait_ge(sem["a%d" % xmem.index(p)], _count(_mask(topo, xmem, p)))
+        tile = col(T.xin, xmem.index(p))
+        mm = ten.matmul(gq, tile, tile, False, j == len(rec) - 1)
+    mm.then_inc(t_gq, 1)
+
+    s_xt16 = new_sem()
+    vec.wait_ge(mc, 1)
+    vec.wait_ge(sem.sxt, 16)
+    vec.tensor_tensor(T.xt16[:, :], T.xts[:, :], T.c16[:, :], mult).then_inc(s_xt16, 1)
+
+    s_i12 = new_sem()
+
+    def constants():
+        s_i6 = new_sem()
+        vec.wait_ge(sem.si3, 16)
+        vec.tensor_tensor(T.i6[:, :], T.i3[:, :], T.i3[:, :], add).then_inc(s_i6, 1)
+        vec.wait_ge(s_i6, 1)
+        vec.tensor_tensor(T.i12[:, :], T.i6[:, :], T.i6[:, :], add).then_inc(s_i12, 1)
+
+    s_a = new_sem()
+    a_sb = T.a_sb[:, :]
+    if not gmem:
+        constants()
+        vec.wait_ge(t_gq, 1)
+        vec.tensor_tensor(a_sb, T.i3[:, :], gq, sub).then_inc(s_a, 1)
+    own, s_own = None, None
+    for k, mem in enumerate(gmem):
+        buf = T["gin%d" % k]
+        name = "b%d_" % k + "%d"
+        final = k == len(gmem) - 1
+        if k == 0:
+            own, s_own = col(buf, mem.index(core)), new_sem()
+            vec.wait_ge(t_gq, 1)
+            vec.tensor_copy(own, gq).then_inc(s_own, 1)
+            part = gq
+        else:
+            part = own
+        g.wait_ge(s_own, 1)
+        send(buf, mem, name)
+        rec = _recv_order(topo, mem, core)
+        vec.wait_ge(s_own, 1)
+        if final:
+            run, s_run = acc_slot(), new_sem()
+            vec.wait_ge(sem.si3, 16)
+            vec.tensor_tensor(run, T.i3[:, :], part, sub).then_inc(s_run, 1)
+            constants()
+            end, s_end, op = a_sb, s_a, sub
+        else:
+            nxt = gmem[k + 1]
+            run, s_run = part, s_own
+            end, s_end, op = col(T["gin%d" % (k + 1)], nxt.index(core)), new_sem(), add
+        for j, p in enumerate(rec):
+            last = j == len(rec) - 1
+            out, s_out = (end, s_end) if last else (acc_slot(), new_sem())
+            vec.wait_ge(s_run, 1)
+            vec.wait_ge(sem[name % mem.index(p)], _count(_mask(topo, mem, p)))
+            vec.tensor_tensor(out, run, col(buf, mem.index(p)), op).then_inc(s_out, 1)
+            run, s_run = out, s_out
+        own, s_own = end, s_end
+
+    s_g, t_b, s_b, t_ut, s_ut, t_c, s_d, t_y, s_y = [new_sem() for j in range(9)]
+    ten.wait_ge(s_a, 1)
+    ten.matmul(T.b_ps[:, 0:P], a_sb, a_sb, True, True).then_inc(t_b, 1)
+    ten.wait_ge(s_xt16, 1)
+    ten.matmul(T.ut_ps[:, 0:P], a_sb, T.xt16[:, :], True, True).then_inc(t_ut, 1)
+    vec.wait_ge(s_a, 1)
+    vec.tensor_tensor(T.g_sb[:, :], T.i3[:, :], a_sb, sub).then_inc(s_g, 1)
+    vec.wait_ge(t_b, 1)
+    vec.tensor_copy(T.b_sb[:, :], T.b_ps[:, 0:P]).then_inc(s_b, 1)
+    ten.wait_ge(s_b, 1)
+    ten.wait_ge(s_g, 1)
+    ten.matmul(T.c_ps[:, 0:P], T.b_sb[:, :], T.g_sb[:, :], True, True).then_inc(t_c, 1)
+    vec.wait_ge(t_ut, 1)
+    vec.tensor_copy(T.ut_sb[:, :], T.ut_ps[:, 0:P]).then_inc(s_ut, 1)
+    vec.wait_ge(t_c, 1)
+    vec.wait_ge(s_i12, 1)
+    vec.tensor_tensor(T.d_sb[:, :], T.i12[:, :], T.c_ps[:, 0:P], sub).then_inc(s_d, 1)
+    ten.wait_ge(s_ut, 1)
+    ten.wait_ge(s_d, 1)
+    ten.matmul(T.y_ps[:, 0:P], T.ut_sb[:, :], T.d_sb[:, :], True, True).then_inc(t_y, 1)
+    vec.wait_ge(t_y, 1)
+    vec.tensor_copy(T.y_sb[:, :], T.y_ps[:, 0:P]).then_inc(s_y, 1)
+    syn.wait_ge(s_y, 1)
+    syn.dma_start(T.y[:, :], T.y_sb[:, :]).then_inc(sem.sout, 16)
+    syn.wait_ge(sem.sout, 16)
+    if left[0]:
+        g.wait_ge(sem.left, left[0])

@@ -2,18 +2,17 @@ from concourse.bass import DstId, RemoteDMATransfer
 from concourse.mybir import AluOpType
 
 P = 128
-SHAPE = ("quad", "trio")
-_SIZE = {"mate": 2, "twin": 2, "trio": 3, "quad": 4, "plane": 6, "all": 12}
-ENGINES = 8
+H = P // 2
+RAW = 2
 
 SCRATCH = {
-    "xin": ("sbuf", [P, P * _SIZE[SHAPE[0]]], "float32"),
+    "xin": ("sbuf", [P, P * 4], "float32"),
+    "gq": ("sbuf", [P, P * 4], "float32"),
+    "gin": ("sbuf", [P, P * 3], "float32"),
     "xts": ("sbuf", [P, P], "float32"),
     "xt16": ("sbuf", [P, P], "float32"),
-    "c16": ("sbuf", [P, P], "float32"),
-    "sd": ("sbuf", [P, P + 1], "float32"),
+    "c3": ("sbuf", [P, P], "float32"),
     "i3": ("sbuf", [P, P], "float32"),
-    "i6": ("sbuf", [P, P], "float32"),
     "i12": ("sbuf", [P, P], "float32"),
     "a_sb": ("sbuf", [P, P], "float32"),
     "g_sb": ("sbuf", [P, P], "float32"),
@@ -21,42 +20,29 @@ SCRATCH = {
     "ut_sb": ("sbuf", [P, P], "float32"),
     "d_sb": ("sbuf", [P, P], "float32"),
     "y_sb": ("sbuf", [P, P], "float32"),
-    "da": ("dram", [P, P + 1], "float32"),
-    "db": ("dram", [P + 1, P], "float32"),
-    "gq": ("psum", [P, 512], "float32"),
+    "g0": ("psum", [P, 512], "float32"),
+    "gx": ("psum", [P, 512], "float32"),
     "acc": ("psum", [P, 512], "float32"),
-    "b_ps": ("psum", [P, 512], "float32"),
+    "ba": ("psum", [P, 512], "float32"),
+    "bb": ("psum", [P, 512], "float32"),
     "ut_ps": ("psum", [P, 512], "float32"),
-    "c_ps": ("psum", [P, 512], "float32"),
-    "y_ps": ("psum", [P, 512], "float32"),
+    "ca": ("psum", [P, 512], "float32"),
+    "cb": ("psum", [P, 512], "float32"),
 }
-SEMAPHORES = ["sx", "sxt", "si3", "sout", "left"]
-SEMAPHORES += ["a%d" % j for j in range(_SIZE[SHAPE[0]])]
-for _k, _kind in enumerate(SHAPE[1:]):
-    SCRATCH["gin%d" % _k] = ("sbuf", [P, P * _SIZE[_kind]], "float32")
-    SEMAPHORES += ["b%d_%d" % (_k, j) for j in range(_SIZE[_kind])]
-SEMAPHORES += ["p%d" % j for j in range(40)]
+SEMAPHORES = ["sx", "sxt", "sout", "left"]
+SEMAPHORES += ["a%d" % j for j in range(4)]
+SEMAPHORES += ["b%d" % j for j in range(3)]
+SEMAPHORES += ["p%d" % j for j in range(32)]
 
 
-def _members(kind, c, ranks, topo):
-    def mate(a):
-        return [r for r in ranks if r == a or topo.mates(a, r)]
+def _quad(c, ranks, topo):
+    pair = [r for r in ranks if r == c or topo.mates(c, r)]
+    both = [r for r in ranks for m in pair if topo.chip(r) == topo.chip(m)]
+    return [r for r in ranks if r in both]
 
-    def twin(a):
-        return [r for r in ranks if topo.chip(r) == topo.chip(a)]
 
-    if kind == "mate":
-        return mate(c)
-    if kind == "twin":
-        return twin(c)
-    if kind == "quad":
-        both = [t for m in mate(c) for t in twin(m)]
-        return [r for r in ranks if r in both]
-    if kind == "trio":
-        return [r for r in ranks if r == c or (topo.same_plane(c, r) and topo.host(r) == topo.host(c))]
-    if kind == "plane":
-        return [r for r in ranks if r == c or topo.same_plane(c, r)]
-    return list(ranks)
+def _trio(c, ranks, topo):
+    return [r for r in ranks if r == c or (topo.same_plane(c, r) and topo.host(r) == topo.host(c))]
 
 
 def _far(topo, a, b):
@@ -82,13 +68,7 @@ def _mask(topo, mem, c):
     for p in mem:
         if p != c:
             m &= topo.mask(c, p)
-    out, bit, n = 0, 1, 0
-    while n < ENGINES and bit <= m:
-        if m & bit:
-            out |= bit
-            n += 1
-        bit <<= 1
-    return out
+    return m
 
 
 def _count(m):
@@ -104,7 +84,6 @@ def rank_program(g, core, T, topo):
     add, sub, mult = AluOpType.add, AluOpType.subtract, AluOpType.mult
     used = [0]
     left = [0]
-    slot = [0]
 
     def new_sem():
         used[0] += 1
@@ -113,14 +92,9 @@ def rank_program(g, core, T, topo):
     def col(buf, j):
         return buf[:, j * P:(j + 1) * P]
 
-    def acc_slot():
-        slot[0] += 1
-        return col(T.acc, (slot[0] - 1) % 4)
-
-    def send(buf, mem, name):
+    def send(buf, mem, peers, name):
         me = mem.index(core)
         m = _mask(topo, mem, core)
-        peers = _send_order(topo, mem, core)
         dests = []
         for p in peers:
             assert topo.may_write(core, p)
@@ -132,120 +106,112 @@ def rank_program(g, core, T, topo):
             local_sem=sem.left)
         left[0] += _count(m)
 
-    xmem = _members(SHAPE[0], core, ranks, topo)
-    gmem = [_members(kind, core, ranks, topo) for kind in SHAPE[1:]]
-    xme = xmem.index(core)
-    xown = col(T.xin, xme)
+    quad = _quad(core, ranks, topo)
+    trio = _trio(core, ranks, topo)
+    qme, tme = quad.index(core), trio.index(core)
+    xown, gown, sown = col(T.xin, qme), col(T.gq, qme), col(T.gin, tme)
+    qsend = _send_order(topo, quad, core)
+    qrecv = _recv_order(topo, quad, core)
+    raw = [p for p in qrecv if core in _send_order(topo, quad, p)[:RAW]]
+    made = [p for p in qrecv if p not in raw]
+    lo, hi = slice(0, H), slice(H, P)
+
+    (m3, t_g0, t_gx, s_gown, s_i3, s_i12, s_xt16, s_sum, s_a, s_g, t_ba, t_bb, s_ba, s_bb, t_ut, s_ut,
+     t_ca, t_cb, s_da, s_db, t_ya, t_yb, s_ya, s_yb) = [new_sem() for j in range(24)]
 
     syn.dma_start(xown, T.x[:, :]).then_inc(sem.sx, 16)
-    m0, m1, mc, d1, d2 = new_sem(), new_sem(), new_sem(), new_sem(), new_sem()
-    vec.memset(T.sd[:, :], 0.0).then_inc(m0, 1)
-    vec.memset(T.c16[:, :], 0.0625).then_inc(mc, 1)
-    vec.wait_ge(m0, 1)
-    vec.memset(T.sd[:, 0:1], 3.0).then_inc(m1, 1)
+    vec.memset(T.c3[:, :], 3.0).then_inc(m3, 1)
     sca.wait_ge(sem.sx, 16)
     sca.dma_start(T.xts[:, :], T.xt[:, :]).then_inc(sem.sxt, 16)
-    sca.wait_ge(m1, 1)
-    sca.dma_start(T.da[:, :], T.sd[:, :]).then_inc(d1, 16)
-    sca.wait_ge(d1, 16)
-    sca.dma_start(T.db[:, :], T.da[:, :]).then_inc(d2, 16)
-    sca.wait_ge(d2, 16)
-    sca.dma_start(T.i3[:, :], T.db[0:P, :]).then_inc(sem.si3, 16)
 
     g.wait_ge(sem.sx, 16)
-    if len(xmem) > 1:
-        send(T.xin, xmem, "a%d")
+    send(T.xin, quad, qsend[:RAW], "a%d")
 
-    t_gq = new_sem()
-    gq = T.gq[:, 0:P]
-    rec = _recv_order(topo, xmem, core)
+    g0, gx = T.g0[:, 0:P], T.gx[:, 0:P]
     ten.wait_ge(sem.sx, 16)
-    mm = ten.matmul(gq, xown, xown, True, not rec)
-    for j, p in enumerate(rec):
-        ten.wait_ge(sem["a%d" % xmem.index(p)], _count(_mask(topo, xmem, p)))
-        tile = col(T.xin, xmem.index(p))
-        mm = ten.matmul(gq, tile, tile, False, j == len(rec) - 1)
-    mm.then_inc(t_gq, 1)
+    ten.matmul(g0, xown, xown, True, True).then_inc(t_g0, 1)
+    mm = ten.matmul(gx, xown, xown, True, not raw)
+    for j, p in enumerate(raw):
+        ten.wait_ge(sem["a%d" % quad.index(p)], _count(_mask(topo, quad, p)))
+        tile = col(T.xin, quad.index(p))
+        mm = ten.matmul(gx, tile, tile, False, j == len(raw) - 1)
+    mm.then_inc(t_gx, 1)
+    vec.wait_ge(t_g0, 1)
+    vec.tensor_copy(gown, g0).then_inc(s_gown, 1)
 
-    s_xt16 = new_sem()
-    vec.wait_ge(mc, 1)
+    g.wait_ge(s_gown, 1)
+    send(T.gq, quad, qsend[RAW:], "a%d")
+
+    g.wait_ge(m3, 1)
+    g.affine_select(T.i3[:, :], T.c3[:, :], [[-1, P]], AluOpType.is_equal, 0.0, 0, 1).then_inc(s_i3, 1)
+
+    run, s_run = gx, t_gx
+    for j, p in enumerate(made):
+        last = j == len(made) - 1
+        out, s_out = (sown, s_sum) if last else (col(T.acc, j), new_sem())
+        vec.wait_ge(sem["a%d" % quad.index(p)], _count(_mask(topo, quad, p)))
+        vec.wait_ge(s_run, 1)
+        vec.tensor_tensor(out, run, col(T.gq, quad.index(p)), add).then_inc(s_out, 1)
+        run, s_run = out, s_out
+
+    g.wait_ge(s_sum, 1)
+    send(T.gin, trio, _send_order(topo, trio, core), "b%d")
+
+    run, s_run = col(T.acc, 2), new_sem()
+    vec.wait_ge(s_sum, 1)
+    vec.wait_ge(s_i3, 1)
+    vec.tensor_tensor(run, T.i3[:, :], sown, sub).then_inc(s_run, 1)
     vec.wait_ge(sem.sxt, 16)
-    vec.tensor_tensor(T.xt16[:, :], T.xts[:, :], T.c16[:, :], mult).then_inc(s_xt16, 1)
-
-    s_i12 = new_sem()
-
-    def constants():
-        s_i6 = new_sem()
-        vec.wait_ge(sem.si3, 16)
-        vec.tensor_tensor(T.i6[:, :], T.i3[:, :], T.i3[:, :], add).then_inc(s_i6, 1)
-        vec.wait_ge(s_i6, 1)
-        vec.tensor_tensor(T.i12[:, :], T.i6[:, :], T.i6[:, :], add).then_inc(s_i12, 1)
-
-    s_a = new_sem()
+    vec.tensor_scalar(T.xt16[:, :], T.xts[:, :], 0.0625, None, mult).then_inc(s_xt16, 1)
+    vec.tensor_scalar(T.i12[:, :], T.i3[:, :], 4.0, None, mult).then_inc(s_i12, 1)
     a_sb = T.a_sb[:, :]
-    if not gmem:
-        constants()
-        vec.wait_ge(t_gq, 1)
-        vec.tensor_tensor(a_sb, T.i3[:, :], gq, sub).then_inc(s_a, 1)
-    own, s_own = None, None
-    for k, mem in enumerate(gmem):
-        buf = T["gin%d" % k]
-        name = "b%d_" % k + "%d"
-        final = k == len(gmem) - 1
-        if k == 0:
-            own, s_own = col(buf, mem.index(core)), new_sem()
-            vec.wait_ge(t_gq, 1)
-            vec.tensor_copy(own, gq).then_inc(s_own, 1)
-            part = gq
-        else:
-            part = own
-        g.wait_ge(s_own, 1)
-        send(buf, mem, name)
-        rec = _recv_order(topo, mem, core)
-        vec.wait_ge(s_own, 1)
-        if final:
-            run, s_run = acc_slot(), new_sem()
-            vec.wait_ge(sem.si3, 16)
-            vec.tensor_tensor(run, T.i3[:, :], part, sub).then_inc(s_run, 1)
-            constants()
-            end, s_end, op = a_sb, s_a, sub
-        else:
-            nxt = gmem[k + 1]
-            run, s_run = part, s_own
-            end, s_end, op = col(T["gin%d" % (k + 1)], nxt.index(core)), new_sem(), add
-        for j, p in enumerate(rec):
-            last = j == len(rec) - 1
-            out, s_out = (end, s_end) if last else (acc_slot(), new_sem())
-            vec.wait_ge(s_run, 1)
-            vec.wait_ge(sem[name % mem.index(p)], _count(_mask(topo, mem, p)))
-            vec.tensor_tensor(out, run, col(buf, mem.index(p)), op).then_inc(s_out, 1)
-            run, s_run = out, s_out
-        own, s_own = end, s_end
+    trecv = _recv_order(topo, trio, core)
+    for j, p in enumerate(trecv):
+        last = j == len(trecv) - 1
+        out, s_out = (a_sb, s_a) if last else (col(T.acc, 3), new_sem())
+        vec.wait_ge(s_run, 1)
+        vec.wait_ge(sem["b%d" % trio.index(p)], _count(_mask(topo, trio, p)))
+        vec.tensor_tensor(out, run, col(T.gin, trio.index(p)), sub).then_inc(s_out, 1)
+        run, s_run = out, s_out
 
-    s_g, t_b, s_b, t_ut, s_ut, t_c, s_d, t_y, s_y = [new_sem() for j in range(9)]
+    ba, bb, ca, cb = T.ba[:, 0:H], T.bb[:, 0:H], T.ca[:, 0:H], T.cb[:, 0:H]
+    ya, yb = T.g0[:, 0:H], T.gx[:, 0:H]
     ten.wait_ge(s_a, 1)
-    ten.matmul(T.b_ps[:, 0:P], a_sb, a_sb, True, True).then_inc(t_b, 1)
+    ten.matmul(ba, a_sb, T.a_sb[:, lo], True, True).then_inc(t_ba, 1)
+    ten.matmul(bb, a_sb, T.a_sb[:, hi], True, True).then_inc(t_bb, 1)
     ten.wait_ge(s_xt16, 1)
     ten.matmul(T.ut_ps[:, 0:P], a_sb, T.xt16[:, :], True, True).then_inc(t_ut, 1)
     vec.wait_ge(s_a, 1)
     vec.tensor_tensor(T.g_sb[:, :], T.i3[:, :], a_sb, sub).then_inc(s_g, 1)
-    vec.wait_ge(t_b, 1)
-    vec.tensor_copy(T.b_sb[:, :], T.b_ps[:, 0:P]).then_inc(s_b, 1)
-    ten.wait_ge(s_b, 1)
+    vec.wait_ge(t_ba, 1)
+    vec.tensor_copy(T.b_sb[:, lo], ba).then_inc(s_ba, 1)
+    vec.wait_ge(t_bb, 1)
+    vec.tensor_copy(T.b_sb[:, hi], bb).then_inc(s_bb, 1)
     ten.wait_ge(s_g, 1)
-    ten.matmul(T.c_ps[:, 0:P], T.b_sb[:, :], T.g_sb[:, :], True, True).then_inc(t_c, 1)
+    ten.wait_ge(s_ba, 1)
+    ten.matmul(ca, T.g_sb[:, :], T.b_sb[:, lo], True, True).then_inc(t_ca, 1)
+    ten.wait_ge(s_bb, 1)
+    ten.matmul(cb, T.g_sb[:, :], T.b_sb[:, hi], True, True).then_inc(t_cb, 1)
     vec.wait_ge(t_ut, 1)
     vec.tensor_copy(T.ut_sb[:, :], T.ut_ps[:, 0:P]).then_inc(s_ut, 1)
-    vec.wait_ge(t_c, 1)
+    vec.wait_ge(t_ca, 1)
     vec.wait_ge(s_i12, 1)
-    vec.tensor_tensor(T.d_sb[:, :], T.i12[:, :], T.c_ps[:, 0:P], sub).then_inc(s_d, 1)
+    vec.tensor_tensor(T.d_sb[:, lo], T.i12[:, lo], ca, sub).then_inc(s_da, 1)
+    vec.wait_ge(t_cb, 1)
+    vec.tensor_tensor(T.d_sb[:, hi], T.i12[:, hi], cb, sub).then_inc(s_db, 1)
+    ten.wait_ge(s_gown, 1)
+    ten.wait_ge(s_sum, 1)
     ten.wait_ge(s_ut, 1)
-    ten.wait_ge(s_d, 1)
-    ten.matmul(T.y_ps[:, 0:P], T.ut_sb[:, :], T.d_sb[:, :], True, True).then_inc(t_y, 1)
-    vec.wait_ge(t_y, 1)
-    vec.tensor_copy(T.y_sb[:, :], T.y_ps[:, 0:P]).then_inc(s_y, 1)
-    syn.wait_ge(s_y, 1)
+    ten.wait_ge(s_da, 1)
+    ten.matmul(ya, T.ut_sb[:, :], T.d_sb[:, lo], True, True).then_inc(t_ya, 1)
+    ten.wait_ge(s_db, 1)
+    ten.matmul(yb, T.ut_sb[:, :], T.d_sb[:, hi], True, True).then_inc(t_yb, 1)
+    vec.wait_ge(t_ya, 1)
+    vec.tensor_copy(T.y_sb[:, lo], ya).then_inc(s_ya, 1)
+    vec.wait_ge(t_yb, 1)
+    vec.tensor_copy(T.y_sb[:, hi], yb).then_inc(s_yb, 1)
+    syn.wait_ge(s_ya, 1)
+    syn.wait_ge(s_yb, 1)
     syn.dma_start(T.y[:, :], T.y_sb[:, :]).then_inc(sem.sout, 16)
     syn.wait_ge(sem.sout, 16)
-    if left[0]:
-        g.wait_ge(sem.left, left[0])
+    g.wait_ge(sem.left, left[0])

from concourse.bass import DstId, RemoteDMATransfer
from concourse.mybir import AluOpType

P = 128
H = P // 2
RAW = 2

SCRATCH = {
    "xin": ("sbuf", [P, P * 4], "float32"),
    "gq": ("sbuf", [P, P * 4], "float32"),
    "gin": ("sbuf", [P, P * 3], "float32"),
    "xts": ("sbuf", [P, P], "float32"),
    "xt16": ("sbuf", [P, P], "float32"),
    "c3": ("sbuf", [P, P], "float32"),
    "i3": ("sbuf", [P, P], "float32"),
    "i12": ("sbuf", [P, P], "float32"),
    "a_sb": ("sbuf", [P, P], "float32"),
    "g_sb": ("sbuf", [P, P], "float32"),
    "b_sb": ("sbuf", [P, P], "float32"),
    "ut_sb": ("sbuf", [P, P], "float32"),
    "d_sb": ("sbuf", [P, P], "float32"),
    "y_sb": ("sbuf", [P, P], "float32"),
    "g0": ("psum", [P, 512], "float32"),
    "gx": ("psum", [P, 512], "float32"),
    "acc": ("psum", [P, 512], "float32"),
    "ba": ("psum", [P, 512], "float32"),
    "bb": ("psum", [P, 512], "float32"),
    "ut_ps": ("psum", [P, 512], "float32"),
    "ca": ("psum", [P, 512], "float32"),
    "cb": ("psum", [P, 512], "float32"),
}
SEMAPHORES = ["sx", "sxt", "sout", "left"]
SEMAPHORES += ["a%d" % j for j in range(4)]
SEMAPHORES += ["b%d" % j for j in range(3)]
SEMAPHORES += ["p%d" % j for j in range(32)]


def _quad(c, ranks, topo):
    pair = [r for r in ranks if r == c or topo.mates(c, r)]
    both = [r for r in ranks for m in pair if topo.chip(r) == topo.chip(m)]
    return [r for r in ranks if r in both]


def _trio(c, ranks, topo):
    return [r for r in ranks if r == c or (topo.same_plane(c, r) and topo.host(r) == topo.host(c))]


def _far(topo, a, b):
    if topo.mates(a, b):
        return 2
    if topo.same_plane(a, b):
        return 1
    return 0


def _send_order(topo, mem, c):
    n = len(mem)
    return sorted([p for p in mem if p != c], key=lambda p: (_far(topo, c, p), (mem.index(p) - mem.index(c)) % n))


def _recv_order(topo, mem, c):
    n = len(mem)
    return sorted([p for p in mem if p != c], key=lambda p: (_far(topo, p, c), (mem.index(c) - mem.index(p)) % n))


def _mask(topo, mem, c):
    m = -1
    for p in mem:
        if p != c:
            m &= topo.mask(c, p)
    return m


def _count(m):
    return bin(m).count("1")


def rank_program(g, core, T, topo):
    if T.rank_of(core) is None:
        return
    ranks = list(T.cores)
    sem = T.sem
    ten, vec, syn, sca = g.tensor, g.vector, g.sync, g.scalar
    add, sub, mult = AluOpType.add, AluOpType.subtract, AluOpType.mult
    used = [0]
    left = [0]

    def new_sem():
        used[0] += 1
        return sem["p%d" % (used[0] - 1)]

    def col(buf, j):
        return buf[:, j * P:(j + 1) * P]

    def send(buf, mem, peers, name):
        me = mem.index(core)
        m = _mask(topo, mem, core)
        dests = []
        for p in peers:
            assert topo.may_write(core, p)
            rid, pid = topo.addr(p, core)
            dests.append(DstId(rid=rid, pnc=pid))
        g.remote_dma_fused(
            [RemoteDMATransfer(dst_ids=dests, dma_engine_mask=m, remote_sem=sem[name % me],
                               srcs=[col(buf, me)], dsts=[col(buf, me) for p in peers])],
            local_sem=sem.left)
        left[0] += _count(m)

    quad = _quad(core, ranks, topo)
    trio = _trio(core, ranks, topo)
    qme, tme = quad.index(core), trio.index(core)
    xown, gown, sown = col(T.xin, qme), col(T.gq, qme), col(T.gin, tme)
    qsend = _send_order(topo, quad, core)
    qrecv = _recv_order(topo, quad, core)
    raw = [p for p in qrecv if core in _send_order(topo, quad, p)[:RAW]]
    made = [p for p in qrecv if p not in raw]
    lo, hi = slice(0, H), slice(H, P)

    (m3, t_g0, t_gx, s_gown, s_i3, s_i12, s_xt16, s_sum, s_a, s_g, t_ba, t_bb, s_ba, s_bb, t_ut, s_ut,
     t_ca, t_cb, s_da, s_db, t_ya, t_yb, s_ya, s_yb) = [new_sem() for j in range(24)]

    syn.dma_start(xown, T.x[:, :]).then_inc(sem.sx, 16)
    vec.memset(T.c3[:, :], 3.0).then_inc(m3, 1)
    sca.wait_ge(sem.sx, 16)
    sca.dma_start(T.xts[:, :], T.xt[:, :]).then_inc(sem.sxt, 16)

    g.wait_ge(sem.sx, 16)
    send(T.xin, quad, qsend[:RAW], "a%d")

    g0, gx = T.g0[:, 0:P], T.gx[:, 0:P]
    ten.wait_ge(sem.sx, 16)
    ten.matmul(g0, xown, xown, True, True).then_inc(t_g0, 1)
    mm = ten.matmul(gx, xown, xown, True, not raw)
    for j, p in enumerate(raw):
        ten.wait_ge(sem["a%d" % quad.index(p)], _count(_mask(topo, quad, p)))
        tile = col(T.xin, quad.index(p))
        mm = ten.matmul(gx, tile, tile, False, j == len(raw) - 1)
    mm.then_inc(t_gx, 1)
    vec.wait_ge(t_g0, 1)
    vec.tensor_copy(gown, g0).then_inc(s_gown, 1)

    g.wait_ge(s_gown, 1)
    send(T.gq, quad, qsend[RAW:], "a%d")

    g.wait_ge(m3, 1)
    g.affine_select(T.i3[:, :], T.c3[:, :], [[-1, P]], AluOpType.is_equal, 0.0, 0, 1).then_inc(s_i3, 1)

    run, s_run = gx, t_gx
    for j, p in enumerate(made):
        last = j == len(made) - 1
        out, s_out = (sown, s_sum) if last else (col(T.acc, j), new_sem())
        vec.wait_ge(sem["a%d" % quad.index(p)], _count(_mask(topo, quad, p)))
        vec.wait_ge(s_run, 1)
        vec.tensor_tensor(out, run, col(T.gq, quad.index(p)), add).then_inc(s_out, 1)
        run, s_run = out, s_out

    g.wait_ge(s_sum, 1)
    send(T.gin, trio, _send_order(topo, trio, core), "b%d")

    run, s_run = col(T.acc, 2), new_sem()
    vec.wait_ge(s_sum, 1)
    vec.wait_ge(s_i3, 1)
    vec.tensor_tensor(run, T.i3[:, :], sown, sub).then_inc(s_run, 1)
    vec.wait_ge(sem.sxt, 16)
    vec.tensor_scalar(T.xt16[:, :], T.xts[:, :], 0.0625, None, mult).then_inc(s_xt16, 1)
    vec.tensor_scalar(T.i12[:, :], T.i3[:, :], 4.0, None, mult).then_inc(s_i12, 1)
    a_sb = T.a_sb[:, :]
    trecv = _recv_order(topo, trio, core)
    for j, p in enumerate(trecv):
        last = j == len(trecv) - 1
        out, s_out = (a_sb, s_a) if last else (col(T.acc, 3), new_sem())
        vec.wait_ge(s_run, 1)
        vec.wait_ge(sem["b%d" % trio.index(p)], _count(_mask(topo, trio, p)))
        vec.tensor_tensor(out, run, col(T.gin, trio.index(p)), sub).then_inc(s_out, 1)
        run, s_run = out, s_out

    ba, bb, ca, cb = T.ba[:, 0:H], T.bb[:, 0:H], T.ca[:, 0:H], T.cb[:, 0:H]
    ya, yb = T.g0[:, 0:H], T.gx[:, 0:H]
    ten.wait_ge(s_a, 1)
    ten.matmul(ba, a_sb, T.a_sb[:, lo], True, True).then_inc(t_ba, 1)
    ten.matmul(bb, a_sb, T.a_sb[:, hi], True, True).then_inc(t_bb, 1)
    ten.wait_ge(s_xt16, 1)
    ten.matmul(T.ut_ps[:, 0:P], a_sb, T.xt16[:, :], True, True).then_inc(t_ut, 1)
    vec.wait_ge(s_a, 1)
    vec.tensor_tensor(T.g_sb[:, :], T.i3[:, :], a_sb, sub).then_inc(s_g, 1)
    vec.wait_ge(t_ba, 1)
    vec.tensor_copy(T.b_sb[:, lo], ba).then_inc(s_ba, 1)
    vec.wait_ge(t_bb, 1)
    vec.tensor_copy(T.b_sb[:, hi], bb).then_inc(s_bb, 1)
    ten.wait_ge(s_g, 1)
    ten.wait_ge(s_ba, 1)
    ten.matmul(ca, T.g_sb[:, :], T.b_sb[:, lo], True, True).then_inc(t_ca, 1)
    ten.wait_ge(s_bb, 1)
    ten.matmul(cb, T.g_sb[:, :], T.b_sb[:, hi], True, True).then_inc(t_cb, 1)
    vec.wait_ge(t_ut, 1)
    vec.tensor_copy(T.ut_sb[:, :], T.ut_ps[:, 0:P]).then_inc(s_ut, 1)
    vec.wait_ge(t_ca, 1)
    vec.wait_ge(s_i12, 1)
    vec.tensor_tensor(T.d_sb[:, lo], T.i12[:, lo], ca, sub).then_inc(s_da, 1)
    vec.wait_ge(t_cb, 1)
    vec.tensor_tensor(T.d_sb[:, hi], T.i12[:, hi], cb, sub).then_inc(s_db, 1)
    ten.wait_ge(s_gown, 1)
    ten.wait_ge(s_sum, 1)
    ten.wait_ge(s_ut, 1)
    ten.wait_ge(s_da, 1)
    ten.matmul(ya, T.ut_sb[:, :], T.d_sb[:, lo], True, True).then_inc(t_ya, 1)
    ten.wait_ge(s_db, 1)
    ten.matmul(yb, T.ut_sb[:, :], T.d_sb[:, hi], True, True).then_inc(t_yb, 1)
    vec.wait_ge(t_ya, 1)
    vec.tensor_copy(T.y_sb[:, lo], ya).then_inc(s_ya, 1)
    vec.wait_ge(t_yb, 1)
    vec.tensor_copy(T.y_sb[:, hi], yb).then_inc(s_yb, 1)
    syn.wait_ge(s_ya, 1)
    syn.wait_ge(s_yb, 1)
    syn.dma_start(T.y[:, :], T.y_sb[:, :]).then_inc(sem.sout, 16)
    syn.wait_ge(sem.sout, 16)
    g.wait_ge(sem.left, left[0])
